import numpy as np
import ml_dtypes


def mxq(x, axis, fmt="e4m3"):
    dtype, down = {"e4m3": (ml_dtypes.float8_e4m3fn, 7), "e5m2": (ml_dtypes.float8_e5m2, 14)}[fmt]
    v = np.moveaxis(np.asarray(x, np.float32).astype(ml_dtypes.bfloat16).astype(np.float64), axis, -1)
    blocks = v.reshape(v.shape[:-1] + (-1, 32))
    amax = np.abs(blocks).max(-1, keepdims=True)
    byte = np.maximum(np.where(amax > 0, np.frexp(amax)[1] - 1 + 127, 0) - down, 1)
    scale = np.exp2(byte - 127.0)
    codes = (blocks / scale).astype(np.float32).astype(dtype).astype(np.float64)
    return np.moveaxis((codes * scale).reshape(v.shape), -1, axis)


WIDE = False


def mx_kscale(k):
    if not WIDE:
        return np.ones(k)
    levels = np.array([10, -10, 5, -5, 0])
    if k % 512:
        return np.exp2(np.random.permutation(np.resize(levels, k // 32))).repeat(32)
    a = np.empty((k // 512, 16))
    for p in range(k // 512):
        a[p, :8] = np.random.permutation(np.resize(levels, 8))
        for g in range(8):
            far = levels[np.abs(levels - a[p, g]) >= 10]
            a[p, g + 8] = far[np.random.randint(len(far))]
    return np.exp2(a.ravel()).repeat(32)


def f64(x):
    return np.asarray(x).astype(np.float64)


def striped8(idx):
    return np.asarray(idx).reshape(8, -1, 16).transpose(0, 2, 1).reshape(128, -1).astype(np.uint16)


def unstriped8(offs):
    return offs.reshape(8, 16, -1).transpose(0, 2, 1).reshape(8, -1).astype(np.int64)


def pick8(x, idx, run):
    r = np.arange(len(x))
    return x[r[:, None], idx[r % (8 * run) // run]]


E2M1 = np.array([0.0, 0.5, 1.0, 1.5, 2.0, 3.0, 4.0, 6.0, -0.0, -0.5, -1.0, -1.5, -2.0, -3.0, -4.0, -6.0])


def pack_weight(w, fmt):
    k, n = w.shape
    w = f64(np.asarray(w, np.float32).astype(ml_dtypes.bfloat16)).reshape(k // 32, 32, n)
    amax = np.abs(w).max(1)
    if fmt == "e4m3":
        byte = np.frexp(amax)[1] - 1 + 127 - 7
    else:
        mant, ex = np.frexp(amax / 6.0)
        byte = np.where(mant > 0.5, ex, ex - 1) + 127
    byte = np.clip(np.where(amax > 0, byte, 1), 1, 254)
    scaled = (w * np.exp2(127.0 - byte)[:, None, :]).reshape(k, n).astype(np.float32)
    by_word = np.ascontiguousarray(scaled.reshape(k // 512, 128, 4, n).transpose(0, 1, 3, 2))
    if fmt == "e4m3":
        words = by_word.astype(ml_dtypes.float8_e4m3fn).view(np.uint8)
    else:
        c = by_word.astype(ml_dtypes.float4_e2m1fn).view(np.uint8) & 0xF
        words = (c[..., 0::2] | (c[..., 1::2] << 4)).reshape(k // 512, 128, 2 * n)
    return np.ascontiguousarray(words), np.ascontiguousarray(byte.astype(np.uint8).reshape(k // 512, 16, n))


def unpack_weight(words, scales, fmt):
    g, _, n = scales.shape
    words = np.ascontiguousarray(words).reshape(g, 128, n, -1)
    if fmt == "e4m3":
        vals = words.view(ml_dtypes.float8_e4m3fn).astype(np.float64)
    else:
        nib = np.empty((g, 128, n, 4), np.uint8)
        nib[..., 0::2] = words & 0xF
        nib[..., 1::2] = words >> 4
        vals = E2M1[nib]
    vals = vals * np.repeat(np.exp2(scales.astype(np.float64) - 127.0), 8, axis=1)[..., None]
    return vals.transpose(0, 1, 3, 2).reshape(g * 512, n)


D, T, I, Q = 512, 1024, 512, 128


def setup_inputs():
    n = np.random.standard_normal
    idx = np.stack([np.random.permutation(T)[:I] for _ in range(8)])
    idx2 = np.stack([np.random.permutation(T)[:I] for _ in range(8)])
    idx3 = np.stack([np.random.permutation(T)[:I] for _ in range(8)])
    fd = mx_kscale(D)
    keysp = pack_weight(n((D, T)) / fd[:, None], "e4m3")
    tagsp = pack_weight(n((D, T)) / fd[:, None], "e2m1")
    return {
        "query": (n((D, Q)) * 0.75 / np.sqrt(D) * fd[:, None]).astype(np.float32),
        "query2": (n((D, Q)) * 0.75 / np.sqrt(D) * fd[:, None]).astype(np.float32),
        "keys_words": keysp[0],
        "keys_scales": keysp[1],
        "tags_words": tagsp[0],
        "tags_scales": tagsp[1],
        "old": (1.0 * n((Q, T))).astype(np.float32),
        "offs": striped8(idx),
        "offs2": striped8(idx2),
        "offs3": striped8(idx3),
    }


def reference(query, query2, keys_words, keys_scales, tags_words, tags_scales, old, offs, offs2, offs3):
    idx = unstriped8(offs)
    idx2 = unstriped8(offs2)
    idx3 = unstriped8(offs3)
    keysu = unpack_weight(keys_words, keys_scales, "e4m3")
    tagsu = unpack_weight(tags_words, tags_scales, "e2m1")
    queryq = mxq(f64(query), 0, "e4m3")
    query2q = mxq(f64(query2), 0, "e4m3")
    a = queryq.T @ keysu + query2q.T @ tagsu
    f1 = np.zeros((Q, T))
    f1[np.arange(Q)[:, None], idx2[np.arange(Q) % 128 // 16]] = pick8(a, idx, 16)
    cc = f64(old) + f1
    tc2 = np.max(cc, axis=1, keepdims=True)
    y = np.exp(pick8(cc, idx3, 16) - tc2)
    return y

@@ -1,0 +1,140 @@
+from contextlib import ExitStack
+
+import concourse.mybir as mybir
+
+D, T, SLOTS, Q = 512, 1024, 512, 128
+FLOPS = 2 * 2 * D * Q * T
+
+F32 = mybir.dt.float32
+BF16 = mybir.dt.bfloat16
+I32 = mybir.dt.int32
+U32 = mybir.dt.uint32
+U16 = mybir.dt.uint16
+U8 = mybir.dt.uint8
+FP8X4 = mybir.dt.float8_e4m3fn_x4
+FP4X4 = mybir.dt.float4_e2m1fn_x4
+ALU = mybir.AluOpType
+ACT = mybir.ActivationFunctionType
+
+P = 128
+PACK = 4
+BANKS = 4
+N = T // BANKS
+HALF = SLOTS // 2
+LIST_COLS = SLOTS // 16
+
+
+def tile_attend_relayed_parts_kernel(
+    tc, query, query2, keys_words, keys_scales, tags_words, tags_scales, old, offs, offs2, offs3, out
+):
+    nc = tc.nc
+    with ExitStack() as ctx:
+        lists = ctx.enter_context(tc.tile_pool(name="lists", bufs=1))
+        sb = ctx.enter_context(tc.tile_pool(name="sb", bufs=1))
+        psum = ctx.enter_context(tc.psum_pool(name="psum", bufs=1))
+
+        pick_list = lists.tile([P, LIST_COLS], U16, name="pick_list")
+        put_list = lists.tile([P, LIST_COLS], U16, name="put_list")
+        fetch_list = lists.tile([P, LIST_COLS], U16, name="fetch_list")
+
+        tags_plane = sb.tile([P, T], U8, name="tags_plane", align_bytes=64)
+        keys_plane = sb.tile([P, T], U8, name="keys_plane", align_bytes=64)
+        relayed = sb.tile([P, T], F32, name="relayed")
+        nc.vector.memset(tags_plane[:].bitcast(U32), 0)
+        nc.vector.memset(keys_plane[:].bitcast(U32), 0)
+        nc.vector.memset(relayed[:], 0.0)
+
+        def load_plane(plane, scales):
+            for quad in range(4):
+                nc.sync.dma_start(
+                    out=plane[32 * quad : 32 * quad + 4, :].bitcast(I32),
+                    in_=scales[0, 4 * quad : 4 * quad + 4, :].bitcast(I32),
+                )
+
+        def load_query(src, name):
+            raw = sb.tile([P, PACK, Q], F32, name=name)
+            nc.sync.dma_start(out=raw[:], in_=src.rearrange("(p j) q -> p j q", j=PACK))
+            return raw
+
+        keys_flat = keys_words[0].rearrange("p n t -> p (n t)")
+
+        def load_keys(h):
+            words = sb.tile([P, T // 2], U32, name="keys_%d" % h, align_bytes=64)
+            nc.sync.dma_start(
+                out=words[:].bitcast(I32), in_=keys_flat[:, h * 2 * T : (h + 1) * 2 * T].bitcast(I32)
+            )
+            return words
+
+        q2_raw = load_query(query2, "q2_raw")
+        nc.sync.dma_start(pick_list[:], offs)
+        load_plane(tags_plane, tags_scales)
+        tags = sb.tile([P, 2 * T], U8, name="tags", align_bytes=64)
+        nc.sync.dma_start(out=tags[:].bitcast(I32), in_=tags_words[0].bitcast(I32))
+        q_raw = load_query(query, "q_raw")
+        keys = [load_keys(0)]
+        load_plane(keys_plane, keys_scales)
+        keys.append(load_keys(1))
+        nc.sync.dma_start(put_list[:], offs2)
+        old_sb = sb.tile([P, T], F32, name="old_sb")
+        nc.sync.dma_start(out=old_sb[:], in_=old)
+        nc.sync.dma_start(fetch_list[:], offs3)
+
+        def quantise(raw, name):
+            woven = sb.tile([P, Q, PACK], BF16, name=name + "_woven", align_bytes=64)
+            nc.vector.tensor_copy(
+                out=woven[:].rearrange("p (c i) t -> p c t i", i=4),
+                in_=raw[:].rearrange("p t (c i) -> p c t i", i=4),
+            )
+            codes = sb.tile([P, Q], U32, name=name + "_codes", align_bytes=64)
+            plane = sb.tile([P, Q], U8, name=name + "_plane", align_bytes=64)
+            nc.vector.quantize_mx(
+                out=codes[:].bitcast(FP8X4), scales=plane[:], in_=woven[:].rearrange("p q t -> p (q t)")
+            )
+            return codes, plane
+
+        q2_codes, q2_plane = quantise(q2_raw, "q2")
+        q_codes, q_plane = quantise(q_raw, "q")
+
+        banks = [psum.tile([P, N], F32, name="bank%d" % b) for b in range(BANKS)]
+        for b in range(BANKS):
+            nc.tensor.matmul_mx(
+                out=banks[b][:],
+                lhsT=q2_codes[:].bitcast(FP8X4),
+                lhsT_scale=q2_plane[:],
+                rhs=tags[:, 2 * b * N : 2 * (b + 1) * N].bitcast(FP4X4),
+                rhs_scale=tags_plane[:, b * N : (b + 1) * N],
+                start=True,
+                stop=False,
+            )
+        scores = sb.tile([P, T], F32, name="scores")
+        for b in range(BANKS):
+            h, r = divmod(b, 2)
+            nc.tensor.matmul_mx(
+                out=banks[b][:],
+                lhsT=q_codes[:].bitcast(FP8X4),
+                lhsT_scale=q_plane[:],
+                rhs=keys[h][:, r * N : (r + 1) * N].bitcast(FP8X4),
+                rhs_scale=keys_plane[:, b * N : (b + 1) * N],
+                start=False,
+                stop=True,
+            )
+            if b % 2 == 0:
+                nc.scalar.activation(scores[:, b * N : (b + 1) * N], banks[b][:], ACT.Copy)
+            else:
+                nc.vector.tensor_copy(out=scores[:, b * N : (b + 1) * N], in_=banks[b][:])
+
+        picked = sb.tile([P, SLOTS], F32, name="picked")
+        nc.vector.tensor_copy(picked[:, :HALF], scores[:].indirect(pick_list[:, : LIST_COLS // 2]))
+        nc.scalar.activation(picked[:, HALF:], scores[:].indirect(pick_list[:, LIST_COLS // 2 :]), ACT.Copy)
+        nc.vector.tensor_copy(relayed[:].indirect(put_list[:]), picked[:])
+
+        totals = sb.tile([P, T], F32, name="totals")
+        nc.vector.tensor_tensor(totals[:], old_sb[:], relayed[:], ALU.add)
+        neg_max = sb.tile([P, 1], F32, name="neg_max")
+        nc.vector.tensor_reduce(neg_max[:], totals[:], mybir.AxisListType.X, ALU.max, negate=True)
+
+        for h in range(2):
+            result = sb.tile([P, HALF], F32, name="result%d" % h)
+            cols = slice(h * LIST_COLS // 2, (h + 1) * LIST_COLS // 2)
+            nc.scalar.activation(result[:], totals[:].indirect(fetch_list[:, cols]), ACT.Exp, bias=neg_max[:])
+            nc.sync.dma_start(out=out[:, h * HALF : (h + 1) * HALF], in_=result[:])

@@ -1,6 +1,7 @@
 from contextlib import ExitStack
 
 import concourse.mybir as mybir
+from concourse.masks import make_identity
 
 D, T, SLOTS, Q = 512, 1024, 512, 128
 FLOPS = 2 * 2 * D * Q * T
@@ -18,8 +19,9 @@ ACT = mybir.ActivationFunctionType
 
 P = 128
 PACK = 4
-BANKS = 4
-N = T // BANKS
+BANK_COLS = [(0, 256), (256, 512), (512, 768), (768, 896), (896, 1024)]
+KEY_LOADS = [(0, 512), (512, 768), (768, 1024)]
+VECTOR_ADDS = [(0, 384), (384, 640)]
 HALF = SLOTS // 2
 LIST_COLS = SLOTS // 16
 
@@ -45,10 +47,10 @@ def tile_attend_relayed_parts_kernel(
         nc.vector.memset(relayed[:], 0.0)
 
         def load_plane(plane, scales):
-            for quad in range(4):
+            for r in range(4):
                 nc.sync.dma_start(
-                    out=plane[32 * quad : 32 * quad + 4, :].bitcast(I32),
-                    in_=scales[0, 4 * quad : 4 * quad + 4, :].bitcast(I32),
+                    out=plane[r:P:32, :].bitcast(I32),
+                    in_=scales[0, r:16:4, :].bitcast(I32),
                 )
 
         def load_query(src, name):
@@ -59,10 +61,9 @@ def tile_attend_relayed_parts_kernel(
         keys_flat = keys_words[0].rearrange("p n t -> p (n t)")
 
         def load_keys(h):
-            words = sb.tile([P, T // 2], U32, name="keys_%d" % h, align_bytes=64)
-            nc.sync.dma_start(
-                out=words[:].bitcast(I32), in_=keys_flat[:, h * 2 * T : (h + 1) * 2 * T].bitcast(I32)
-            )
+            lo, hi = KEY_LOADS[h]
+            words = sb.tile([P, hi - lo], U32, name="keys_%d" % h, align_bytes=64)
+            nc.sync.dma_start(out=words[:].bitcast(I32), in_=keys_flat[:, PACK * lo : PACK * hi].bitcast(I32))
             return words
 
         q2_raw = load_query(query2, "q2_raw")
@@ -71,67 +72,92 @@ def tile_attend_relayed_parts_kernel(
         tags = sb.tile([P, 2 * T], U8, name="tags", align_bytes=64)
         nc.sync.dma_start(out=tags[:].bitcast(I32), in_=tags_words[0].bitcast(I32))
         q_raw = load_query(query, "q_raw")
-        keys = [load_keys(0)]
         load_plane(keys_plane, keys_scales)
-        keys.append(load_keys(1))
+        keys = [load_keys(h) for h in range(len(KEY_LOADS))]
         nc.sync.dma_start(put_list[:], offs2)
         old_sb = sb.tile([P, T], F32, name="old_sb")
         nc.sync.dma_start(out=old_sb[:], in_=old)
         nc.sync.dma_start(fetch_list[:], offs3)
 
         def quantise(raw, name):
-            woven = sb.tile([P, Q, PACK], BF16, name=name + "_woven", align_bytes=64)
-            nc.vector.tensor_copy(
-                out=woven[:].rearrange("p (c i) t -> p c t i", i=4),
-                in_=raw[:].rearrange("p t (c i) -> p c t i", i=4),
-            )
             codes = sb.tile([P, Q], U32, name=name + "_codes", align_bytes=64)
             plane = sb.tile([P, Q], U8, name=name + "_plane", align_bytes=64)
-            nc.vector.quantize_mx(
-                out=codes[:].bitcast(FP8X4), scales=plane[:], in_=woven[:].rearrange("p q t -> p (q t)")
-            )
+            halves = [slice(0, Q // 2), slice(Q // 2, Q)]
+            woven = [sb.tile([P, Q // 2, PACK], BF16, name=name + "_woven%d" % h, align_bytes=64) for h in range(2)]
+            for h in range(2):
+                nc.vector.tensor_copy(
+                    out=woven[h][:].rearrange("p (c i) t -> p c t i", i=4),
+                    in_=raw[:, :, halves[h]].rearrange("p t (c i) -> p c t i", i=4),
+                )
+            for h in range(2):
+                nc.vector.quantize_mx(
+                    out=codes[:, halves[h]].bitcast(FP8X4),
+                    scales=plane[:, halves[h]],
+                    in_=woven[h][:].rearrange("p q t -> p (q t)"),
+                )
             return codes, plane
 
         q2_codes, q2_plane = quantise(q2_raw, "q2")
         q_codes, q_plane = quantise(q_raw, "q")
 
-        banks = [psum.tile([P, N], F32, name="bank%d" % b) for b in range(BANKS)]
-        for b in range(BANKS):
+        banks = [psum.tile([P, hi - lo], F32, name="bank%d" % b) for b, (lo, hi) in enumerate(BANK_COLS)]
+        for b, (lo, hi) in enumerate(BANK_COLS):
             nc.tensor.matmul_mx(
                 out=banks[b][:],
                 lhsT=q2_codes[:].bitcast(FP8X4),
                 lhsT_scale=q2_plane[:],
-                rhs=tags[:, 2 * b * N : 2 * (b + 1) * N].bitcast(FP4X4),
-                rhs_scale=tags_plane[:, b * N : (b + 1) * N],
+                rhs=tags[:, 2 * lo : 2 * hi].bitcast(FP4X4),
+                rhs_scale=tags_plane[:, lo:hi],
                 start=True,
                 stop=False,
             )
         scores = sb.tile([P, T], F32, name="scores")
-        for b in range(BANKS):
-            h, r = divmod(b, 2)
+        for b, (lo, hi) in enumerate(BANK_COLS):
+            h = min(i for i, span in enumerate(KEY_LOADS) if hi <= span[1])
+            base = KEY_LOADS[h][0]
             nc.tensor.matmul_mx(
                 out=banks[b][:],
                 lhsT=q_codes[:].bitcast(FP8X4),
                 lhsT_scale=q_plane[:],
-                rhs=keys[h][:, r * N : (r + 1) * N].bitcast(FP8X4),
-                rhs_scale=keys_plane[:, b * N : (b + 1) * N],
+                rhs=keys[h][:, lo - base : hi - base].bitcast(FP8X4),
+                rhs_scale=keys_plane[:, lo:hi],
                 start=False,
                 stop=True,
             )
-            if b % 2 == 0:
-                nc.scalar.activation(scores[:, b * N : (b + 1) * N], banks[b][:], ACT.Copy)
+            if b % 2 == 1:
+                nc.scalar.activation(scores[:, lo:hi], banks[b][:], ACT.Copy)
             else:
-                nc.vector.tensor_copy(out=scores[:, b * N : (b + 1) * N], in_=banks[b][:])
+                nc.vector.tensor_copy(out=scores[:, lo:hi], in_=banks[b][:])
 
         picked = sb.tile([P, SLOTS], F32, name="picked")
         nc.vector.tensor_copy(picked[:, :HALF], scores[:].indirect(pick_list[:, : LIST_COLS // 2]))
         nc.scalar.activation(picked[:, HALF:], scores[:].indirect(pick_list[:, LIST_COLS // 2 :]), ACT.Copy)
         nc.vector.tensor_copy(relayed[:].indirect(put_list[:]), picked[:])
 
-        totals = sb.tile([P, T], F32, name="totals")
-        nc.vector.tensor_tensor(totals[:], old_sb[:], relayed[:], ALU.add)
+        ident = sb.tile([P, P], F32, name="ident", tag="q_woven1", align_bytes=64)
+        make_identity(nc, ident[:])
+        old_banks = []
+        turned_sb = sb.tile([P, VECTOR_ADDS[-1][1]], F32, name="turned_sb", tag="totals")
+        for n, (lo, hi) in enumerate(VECTOR_ADDS):
+            turned = psum.tile([P, hi - lo], F32, name="turned%d" % n, tag="bank%d" % (3 + n))
+            for c in range(0, hi - lo, P):
+                nc.tensor.transpose(turned[:, c : c + P], old_sb[:, lo + c : lo + c + P], ident[:])
+            nc.scalar.copy(turned_sb[:, lo:hi], turned[:])
+            back = psum.tile([P, hi - lo], F32, name="old_bank%d" % n)
+            for c in range(0, hi - lo, P):
+                nc.tensor.transpose(back[:, c : c + P], turned_sb[:, lo + c : lo + c + P], ident[:])
+            old_banks.append(back)
+
+        totals = sb.tile([P, T], F32, name="totals", tag="totals")
+        rest = VECTOR_ADDS[-1][1]
+        for n, (lo, hi) in enumerate(VECTOR_ADDS):
+            nc.vector.tensor_tensor(totals[:, lo:hi], old_banks[n][:], relayed[:, lo:hi], ALU.add)
+        nc.gpsimd.tensor_tensor(totals[:, rest:], old_sb[:, rest:], relayed[:, rest:], ALU.add)
+        part_max = sb.tile([P, 3], F32, name="part_max")
+        for n, (lo, hi) in enumerate(VECTOR_ADDS + [(rest, T)]):
+            nc.vector.tensor_reduce(part_max[:, n : n + 1], totals[:, lo:hi], mybir.AxisListType.X, ALU.max)
         neg_max = sb.tile([P, 1], F32, name="neg_max")
-        nc.vector.tensor_reduce(neg_max[:], totals[:], mybir.AxisListType.X, ALU.max, negate=True)
+        nc.vector.tensor_reduce(neg_max[:], part_max[:], mybir.AxisListType.X, ALU.max, negate=True)
 
         for h in range(2):
             result = sb.tile([P, HALF], F32, name="result%d" % h)

@@ -66,17 +66,26 @@ def tile_attend_relayed_parts_kernel(
             nc.sync.dma_start(out=words[:].bitcast(I32), in_=keys_flat[:, PACK * lo : PACK * hi].bitcast(I32))
             return words
 
+        def load_tags(h):
+            words = sb.tile([P, T], U8, name="tags_%d" % h, align_bytes=64)
+            nc.sync.dma_start(out=words[:].bitcast(I32), in_=tags_words[0][:, h * T : (h + 1) * T].bitcast(I32))
+            return words
+
         q2_raw = load_query(query2, "q2_raw")
-        nc.sync.dma_start(pick_list[:], offs)
+        tags = [load_tags(0)]
         load_plane(tags_plane, tags_scales)
-        tags = sb.tile([P, 2 * T], U8, name="tags", align_bytes=64)
-        nc.sync.dma_start(out=tags[:].bitcast(I32), in_=tags_words[0].bitcast(I32))
+        tags.append(load_tags(1))
         q_raw = load_query(query, "q_raw")
+        keys = [load_keys(0)]
         load_plane(keys_plane, keys_scales)
-        keys = [load_keys(h) for h in range(len(KEY_LOADS))]
+        keys.extend(load_keys(h) for h in range(1, len(KEY_LOADS)))
+        nc.sync.dma_start(pick_list[:], offs)
         nc.sync.dma_start(put_list[:], offs2)
-        old_sb = sb.tile([P, T], F32, name="old_sb")
-        nc.sync.dma_start(out=old_sb[:], in_=old)
+        rest = VECTOR_ADDS[-1][1]
+        old_sb = sb.tile([P, rest], F32, name="old_sb")
+        nc.sync.dma_start(out=old_sb[:], in_=old[:, :rest])
+        old_rest = sb.tile([P, T - rest], F32, name="old_rest")
+        nc.sync.dma_start(out=old_rest[:], in_=old[:, rest:])
         nc.sync.dma_start(fetch_list[:], offs3)
 
         def quantise(raw, name):
@@ -106,7 +115,7 @@ def tile_attend_relayed_parts_kernel(
                 out=banks[b][:],
                 lhsT=q2_codes[:].bitcast(FP8X4),
                 lhsT_scale=q2_plane[:],
-                rhs=tags[:, 2 * lo : 2 * hi].bitcast(FP4X4),
+                rhs=tags[lo // 512][:, 2 * (lo % 512) : 2 * (lo % 512 + hi - lo)].bitcast(FP4X4),
                 rhs_scale=tags_plane[:, lo:hi],
                 start=True,
                 stop=False,
@@ -149,10 +158,9 @@ def tile_attend_relayed_parts_kernel(
             old_banks.append(back)
 
         totals = sb.tile([P, T], F32, name="totals", tag="totals")
-        rest = VECTOR_ADDS[-1][1]
         for n, (lo, hi) in enumerate(VECTOR_ADDS):
             nc.vector.tensor_tensor(totals[:, lo:hi], old_banks[n][:], relayed[:, lo:hi], ALU.add)
-        nc.gpsimd.tensor_tensor(totals[:, rest:], old_sb[:, rest:], relayed[:, rest:], ALU.add)
+        nc.gpsimd.tensor_tensor(totals[:, rest:], old_rest[:], relayed[:, rest:], ALU.add)
         part_max = sb.tile([P, 3], F32, name="part_max")
         for n, (lo, hi) in enumerate(VECTOR_ADDS + [(rest, T)]):
             nc.vector.tensor_reduce(part_max[:, n : n + 1], totals[:, lo:hi], mybir.AxisListType.X, ALU.max)

@@ -16,14 +16,20 @@ FP8X4 = mybir.dt.float8_e4m3fn_x4
 FP4X4 = mybir.dt.float4_e2m1fn_x4
 ALU = mybir.AluOpType
 ACT = mybir.ActivationFunctionType
+FREE_AXIS = mybir.AxisListType.X
 
 P = 128
 PACK = 4
+QUADRANT = 32
+SCALE_ROWS = 4
+HALF = SLOTS // 2
+LIST_COLS = SLOTS // 16
+HALF_LIST = [slice(0, LIST_COLS // 2), slice(LIST_COLS // 2, LIST_COLS)]
+
 BANK_COLS = [(0, 256), (256, 512), (512, 768), (768, 896), (896, 1024)]
 KEY_LOADS = [(0, 512), (512, 768), (768, 1024)]
 VECTOR_ADDS = [(0, 384), (384, 640)]
-HALF = SLOTS // 2
-LIST_COLS = SLOTS // 16
+GPSIMD_ADD = (VECTOR_ADDS[-1][1], T)
 
 
 def tile_attend_relayed_parts_kernel(
@@ -46,46 +52,44 @@ def tile_attend_relayed_parts_kernel(
         nc.vector.memset(keys_plane[:].bitcast(U32), 0)
         nc.vector.memset(relayed[:], 0.0)
 
-        def load_plane(plane, scales):
-            for r in range(4):
-                nc.sync.dma_start(
-                    out=plane[r:P:32, :].bitcast(I32),
-                    in_=scales[0, r:16:4, :].bitcast(I32),
+        def load_plane(plane, scales, queues):
+            for r in range(SCALE_ROWS):
+                queues[r % len(queues)].dma_start(
+                    out=plane[r:P:QUADRANT, :].bitcast(I32),
+                    in_=scales[0, r : D // 32 : SCALE_ROWS, :].bitcast(I32),
                 )
 
-        def load_query(src, name):
+        def load_query(src, name, parts):
             raw = sb.tile([P, PACK, Q], F32, name=name)
-            nc.sync.dma_start(out=raw[:], in_=src.rearrange("(p j) q -> p j q", j=PACK))
+            rows = src.rearrange("(p j) q -> p j q", j=PACK)
+            step = PACK // parts
+            for j in range(0, PACK, step):
+                nc.sync.dma_start(out=raw[:, j : j + step, :], in_=rows[:, j : j + step, :])
             return raw
 
         keys_flat = keys_words[0].rearrange("p n t -> p (n t)")
 
-        def load_keys(h):
-            lo, hi = KEY_LOADS[h]
-            words = sb.tile([P, hi - lo], U32, name="keys_%d" % h, align_bytes=64)
+        def load_keys(n):
+            lo, hi = KEY_LOADS[n]
+            words = sb.tile([P, hi - lo], U32, name="keys_%d" % n, align_bytes=64)
             nc.sync.dma_start(out=words[:].bitcast(I32), in_=keys_flat[:, PACK * lo : PACK * hi].bitcast(I32))
             return words
 
-        def load_tags(h):
-            words = sb.tile([P, T], U8, name="tags_%d" % h, align_bytes=64)
-            nc.sync.dma_start(out=words[:].bitcast(I32), in_=tags_words[0][:, h * T : (h + 1) * T].bitcast(I32))
-            return words
-
-        q2_raw = load_query(query2, "q2_raw")
-        tags = [load_tags(0)]
-        load_plane(tags_plane, tags_scales)
-        tags.append(load_tags(1))
-        q_raw = load_query(query, "q_raw")
+        q2_raw = load_query(query2, "q2_raw", 2)
+        load_plane(tags_plane, tags_scales, [nc.sync, nc.scalar])
+        tags = sb.tile([P, 2 * T], U8, name="tags", align_bytes=64)
+        nc.sync.dma_start(out=tags[:].bitcast(I32), in_=tags_words[0].bitcast(I32))
+        q_raw = load_query(query, "q_raw", 1)
         keys = [load_keys(0)]
-        load_plane(keys_plane, keys_scales)
-        keys.extend(load_keys(h) for h in range(1, len(KEY_LOADS)))
+        load_plane(keys_plane, keys_scales, [nc.sync])
+        keys.extend(load_keys(n) for n in range(1, len(KEY_LOADS)))
         nc.sync.dma_start(pick_list[:], offs)
         nc.sync.dma_start(put_list[:], offs2)
-        rest = VECTOR_ADDS[-1][1]
-        old_sb = sb.tile([P, rest], F32, name="old_sb")
-        nc.sync.dma_start(out=old_sb[:], in_=old[:, :rest])
-        old_rest = sb.tile([P, T - rest], F32, name="old_rest")
-        nc.sync.dma_start(out=old_rest[:], in_=old[:, rest:])
+        split = GPSIMD_ADD[0]
+        old_vector = sb.tile([P, split], F32, name="old_vector")
+        nc.sync.dma_start(out=old_vector[:], in_=old[:, :split])
+        old_gpsimd = sb.tile([P, T - split], F32, name="old_gpsimd")
+        nc.sync.dma_start(out=old_gpsimd[:], in_=old[:, split:])
         nc.sync.dma_start(fetch_list[:], offs3)
 
         def quantise(raw, name):
@@ -95,14 +99,14 @@ def tile_attend_relayed_parts_kernel(
             woven = [sb.tile([P, Q // 2, PACK], BF16, name=name + "_woven%d" % h, align_bytes=64) for h in range(2)]
             for h in range(2):
                 nc.vector.tensor_copy(
-                    out=woven[h][:].rearrange("p (c i) t -> p c t i", i=4),
-                    in_=raw[:, :, halves[h]].rearrange("p t (c i) -> p c t i", i=4),
+                    out=woven[h][:].rearrange("p (c i) j -> p c j i", i=4),
+                    in_=raw[:, :, halves[h]].rearrange("p j (c i) -> p c j i", i=4),
                 )
             for h in range(2):
                 nc.vector.quantize_mx(
                     out=codes[:, halves[h]].bitcast(FP8X4),
                     scales=plane[:, halves[h]],
-                    in_=woven[h][:].rearrange("p q t -> p (q t)"),
+                    in_=woven[h][:].rearrange("p q j -> p (q j)"),
                 )
             return codes, plane
 
@@ -115,20 +119,20 @@ def tile_attend_relayed_parts_kernel(
                 out=banks[b][:],
                 lhsT=q2_codes[:].bitcast(FP8X4),
                 lhsT_scale=q2_plane[:],
-                rhs=tags[lo // 512][:, 2 * (lo % 512) : 2 * (lo % 512 + hi - lo)].bitcast(FP4X4),
+                rhs=tags[:, 2 * lo : 2 * hi].bitcast(FP4X4),
                 rhs_scale=tags_plane[:, lo:hi],
                 start=True,
                 stop=False,
             )
         scores = sb.tile([P, T], F32, name="scores")
         for b, (lo, hi) in enumerate(BANK_COLS):
-            h = min(i for i, span in enumerate(KEY_LOADS) if hi <= span[1])
-            base = KEY_LOADS[h][0]
+            n = min(i for i, span in enumerate(KEY_LOADS) if hi <= span[1])
+            base = KEY_LOADS[n][0]
             nc.tensor.matmul_mx(
                 out=banks[b][:],
                 lhsT=q_codes[:].bitcast(FP8X4),
                 lhsT_scale=q_plane[:],
-                rhs=keys[h][:, lo - base : hi - base].bitcast(FP8X4),
+                rhs=keys[n][:, lo - base : hi - base].bitcast(FP8X4),
                 rhs_scale=keys_plane[:, lo:hi],
                 start=False,
                 stop=True,
@@ -139,36 +143,40 @@ def tile_attend_relayed_parts_kernel(
                 nc.vector.tensor_copy(out=scores[:, lo:hi], in_=banks[b][:])
 
         picked = sb.tile([P, SLOTS], F32, name="picked")
-        nc.vector.tensor_copy(picked[:, :HALF], scores[:].indirect(pick_list[:, : LIST_COLS // 2]))
-        nc.scalar.activation(picked[:, HALF:], scores[:].indirect(pick_list[:, LIST_COLS // 2 :]), ACT.Copy)
+        nc.vector.tensor_copy(picked[:, :HALF], scores[:].indirect(pick_list[:, HALF_LIST[0]]))
+        nc.scalar.activation(picked[:, HALF:], scores[:].indirect(pick_list[:, HALF_LIST[1]]), ACT.Copy)
         nc.vector.tensor_copy(relayed[:].indirect(put_list[:]), picked[:])
 
         ident = sb.tile([P, P], F32, name="ident", tag="q_woven1", align_bytes=64)
         make_identity(nc, ident[:])
         old_banks = []
-        turned_sb = sb.tile([P, VECTOR_ADDS[-1][1]], F32, name="turned_sb", tag="totals")
+        turned_sb = sb.tile([P, split], F32, name="turned_sb", tag="totals")
         for n, (lo, hi) in enumerate(VECTOR_ADDS):
-            turned = psum.tile([P, hi - lo], F32, name="turned%d" % n, tag="bank%d" % (3 + n))
+            last_banks = len(BANK_COLS) - len(VECTOR_ADDS)
+            turned = psum.tile([P, hi - lo], F32, name="turned%d" % n, tag="bank%d" % (last_banks + n))
             for c in range(0, hi - lo, P):
-                nc.tensor.transpose(turned[:, c : c + P], old_sb[:, lo + c : lo + c + P], ident[:])
+                nc.tensor.transpose(turned[:, c : c + P], old_vector[:, lo + c : lo + c + P], ident[:])
             nc.scalar.copy(turned_sb[:, lo:hi], turned[:])
-            back = psum.tile([P, hi - lo], F32, name="old_bank%d" % n)
+            old_bank = psum.tile([P, hi - lo], F32, name="old_bank%d" % n)
             for c in range(0, hi - lo, P):
-                nc.tensor.transpose(back[:, c : c + P], turned_sb[:, lo + c : lo + c + P], ident[:])
-            old_banks.append(back)
+                nc.tensor.transpose(old_bank[:, c : c + P], turned_sb[:, lo + c : lo + c + P], ident[:])
+            old_banks.append(old_bank)
 
         totals = sb.tile([P, T], F32, name="totals", tag="totals")
         for n, (lo, hi) in enumerate(VECTOR_ADDS):
             nc.vector.tensor_tensor(totals[:, lo:hi], old_banks[n][:], relayed[:, lo:hi], ALU.add)
-        nc.gpsimd.tensor_tensor(totals[:, rest:], old_rest[:], relayed[:, rest:], ALU.add)
-        part_max = sb.tile([P, 3], F32, name="part_max")
-        for n, (lo, hi) in enumerate(VECTOR_ADDS + [(rest, T)]):
-            nc.vector.tensor_reduce(part_max[:, n : n + 1], totals[:, lo:hi], mybir.AxisListType.X, ALU.max)
+        nc.gpsimd.tensor_tensor(totals[:, split:], old_gpsimd[:], relayed[:, split:], ALU.add)
+
+        shares = VECTOR_ADDS + [GPSIMD_ADD]
+        share_max = sb.tile([P, len(shares)], F32, name="share_max")
+        for n, (lo, hi) in enumerate(shares):
+            nc.vector.tensor_reduce(share_max[:, n : n + 1], totals[:, lo:hi], FREE_AXIS, ALU.max)
         neg_max = sb.tile([P, 1], F32, name="neg_max")
-        nc.vector.tensor_reduce(neg_max[:], part_max[:], mybir.AxisListType.X, ALU.max, negate=True)
+        nc.vector.tensor_reduce(neg_max[:], share_max[:], FREE_AXIS, ALU.max, negate=True)
 
         for h in range(2):
             result = sb.tile([P, HALF], F32, name="result%d" % h)
-            cols = slice(h * LIST_COLS // 2, (h + 1) * LIST_COLS // 2)
-            nc.scalar.activation(result[:], totals[:].indirect(fetch_list[:, cols]), ACT.Exp, bias=neg_max[:])
+            nc.scalar.activation(
+                result[:], totals[:].indirect(fetch_list[:, HALF_LIST[h]]), ACT.Exp, bias=neg_max[:]
+            )
             nc.sync.dma_start(out=out[:, h * HALF : (h + 1) * HALF], in_=result[:])

from contextlib import ExitStack

import concourse.mybir as mybir
from concourse.masks import make_identity

D, T, SLOTS, Q = 512, 1024, 512, 128
FLOPS = 2 * 2 * D * Q * T

F32 = mybir.dt.float32
BF16 = mybir.dt.bfloat16
I32 = mybir.dt.int32
U32 = mybir.dt.uint32
U16 = mybir.dt.uint16
U8 = mybir.dt.uint8
FP8X4 = mybir.dt.float8_e4m3fn_x4
FP4X4 = mybir.dt.float4_e2m1fn_x4
ALU = mybir.AluOpType
ACT = mybir.ActivationFunctionType
FREE_AXIS = mybir.AxisListType.X

P = 128
PACK = 4
QUADRANT = 32
SCALE_ROWS = 4
HALF = SLOTS // 2
LIST_COLS = SLOTS // 16
HALF_LIST = [slice(0, LIST_COLS // 2), slice(LIST_COLS // 2, LIST_COLS)]

BANK_COLS = [(0, 256), (256, 512), (512, 768), (768, 896), (896, 1024)]
KEY_LOADS = [(0, 512), (512, 768), (768, 1024)]
VECTOR_ADDS = [(0, 384), (384, 640)]
GPSIMD_ADD = (VECTOR_ADDS[-1][1], T)


def tile_attend_relayed_parts_kernel(
    tc, query, query2, keys_words, keys_scales, tags_words, tags_scales, old, offs, offs2, offs3, out
):
    nc = tc.nc
    with ExitStack() as ctx:
        lists = ctx.enter_context(tc.tile_pool(name="lists", bufs=1))
        sb = ctx.enter_context(tc.tile_pool(name="sb", bufs=1))
        psum = ctx.enter_context(tc.psum_pool(name="psum", bufs=1))

        pick_list = lists.tile([P, LIST_COLS], U16, name="pick_list")
        put_list = lists.tile([P, LIST_COLS], U16, name="put_list")
        fetch_list = lists.tile([P, LIST_COLS], U16, name="fetch_list")

        tags_plane = sb.tile([P, T], U8, name="tags_plane", align_bytes=64)
        keys_plane = sb.tile([P, T], U8, name="keys_plane", align_bytes=64)
        relayed = sb.tile([P, T], F32, name="relayed")
        nc.vector.memset(tags_plane[:].bitcast(U32), 0)
        nc.vector.memset(keys_plane[:].bitcast(U32), 0)
        nc.vector.memset(relayed[:], 0.0)

        def load_plane(plane, scales, queues):
            for r in range(SCALE_ROWS):
                queues[r % len(queues)].dma_start(
                    out=plane[r:P:QUADRANT, :].bitcast(I32),
                    in_=scales[0, r : D // 32 : SCALE_ROWS, :].bitcast(I32),
                )

        def load_query(src, name, parts):
            raw = sb.tile([P, PACK, Q], F32, name=name)
            rows = src.rearrange("(p j) q -> p j q", j=PACK)
            step = PACK // parts
            for j in range(0, PACK, step):
                nc.sync.dma_start(out=raw[:, j : j + step, :], in_=rows[:, j : j + step, :])
            return raw

        keys_flat = keys_words[0].rearrange("p n t -> p (n t)")

        def load_keys(n):
            lo, hi = KEY_LOADS[n]
            words = sb.tile([P, hi - lo], U32, name="keys_%d" % n, align_bytes=64)
            nc.sync.dma_start(out=words[:].bitcast(I32), in_=keys_flat[:, PACK * lo : PACK * hi].bitcast(I32))
            return words

        q2_raw = load_query(query2, "q2_raw", 2)
        load_plane(tags_plane, tags_scales, [nc.sync, nc.scalar])
        tags = sb.tile([P, 2 * T], U8, name="tags", align_bytes=64)
        nc.sync.dma_start(out=tags[:].bitcast(I32), in_=tags_words[0].bitcast(I32))
        q_raw = load_query(query, "q_raw", 1)
        keys = [load_keys(0)]
        load_plane(keys_plane, keys_scales, [nc.sync])
        keys.extend(load_keys(n) for n in range(1, len(KEY_LOADS)))
        nc.sync.dma_start(pick_list[:], offs)
        nc.sync.dma_start(put_list[:], offs2)
        split = GPSIMD_ADD[0]
        old_vector = sb.tile([P, split], F32, name="old_vector")
        nc.sync.dma_start(out=old_vector[:], in_=old[:, :split])
        old_gpsimd = sb.tile([P, T - split], F32, name="old_gpsimd")
        nc.sync.dma_start(out=old_gpsimd[:], in_=old[:, split:])
        nc.sync.dma_start(fetch_list[:], offs3)

        def quantise(raw, name):
            codes = sb.tile([P, Q], U32, name=name + "_codes", align_bytes=64)
            plane = sb.tile([P, Q], U8, name=name + "_plane", align_bytes=64)
            halves = [slice(0, Q // 2), slice(Q // 2, Q)]
            woven = [sb.tile([P, Q // 2, PACK], BF16, name=name + "_woven%d" % h, align_bytes=64) for h in range(2)]
            for h in range(2):
                nc.vector.tensor_copy(
                    out=woven[h][:].rearrange("p (c i) j -> p c j i", i=4),
                    in_=raw[:, :, halves[h]].rearrange("p j (c i) -> p c j i", i=4),
                )
            for h in range(2):
                nc.vector.quantize_mx(
                    out=codes[:, halves[h]].bitcast(FP8X4),
                    scales=plane[:, halves[h]],
                    in_=woven[h][:].rearrange("p q j -> p (q j)"),
                )
            return codes, plane

        q2_codes, q2_plane = quantise(q2_raw, "q2")
        q_codes, q_plane = quantise(q_raw, "q")

        banks = [psum.tile([P, hi - lo], F32, name="bank%d" % b) for b, (lo, hi) in enumerate(BANK_COLS)]
        for b, (lo, hi) in enumerate(BANK_COLS):
            nc.tensor.matmul_mx(
                out=banks[b][:],
                lhsT=q2_codes[:].bitcast(FP8X4),
                lhsT_scale=q2_plane[:],
                rhs=tags[:, 2 * lo : 2 * hi].bitcast(FP4X4),
                rhs_scale=tags_plane[:, lo:hi],
                start=True,
                stop=False,
            )
        scores = sb.tile([P, T], F32, name="scores")
        for b, (lo, hi) in enumerate(BANK_COLS):
            n = min(i for i, span in enumerate(KEY_LOADS) if hi <= span[1])
            base = KEY_LOADS[n][0]
            nc.tensor.matmul_mx(
                out=banks[b][:],
                lhsT=q_codes[:].bitcast(FP8X4),
                lhsT_scale=q_plane[:],
                rhs=keys[n][:, lo - base : hi - base].bitcast(FP8X4),
                rhs_scale=keys_plane[:, lo:hi],
                start=False,
                stop=True,
            )
            if b % 2 == 1:
                nc.scalar.activation(scores[:, lo:hi], banks[b][:], ACT.Copy)
            else:
                nc.vector.tensor_copy(out=scores[:, lo:hi], in_=banks[b][:])

        picked = sb.tile([P, SLOTS], F32, name="picked")
        nc.vector.tensor_copy(picked[:, :HALF], scores[:].indirect(pick_list[:, HALF_LIST[0]]))
        nc.scalar.activation(picked[:, HALF:], scores[:].indirect(pick_list[:, HALF_LIST[1]]), ACT.Copy)
        nc.vector.tensor_copy(relayed[:].indirect(put_list[:]), picked[:])

        ident = sb.tile([P, P], F32, name="ident", tag="q_woven1", align_bytes=64)
        make_identity(nc, ident[:])
        old_banks = []
        turned_sb = sb.tile([P, split], F32, name="turned_sb", tag="totals")
        for n, (lo, hi) in enumerate(VECTOR_ADDS):
            last_banks = len(BANK_COLS) - len(VECTOR_ADDS)
            turned = psum.tile([P, hi - lo], F32, name="turned%d" % n, tag="bank%d" % (last_banks + n))
            for c in range(0, hi - lo, P):
                nc.tensor.transpose(turned[:, c : c + P], old_vector[:, lo + c : lo + c + P], ident[:])
            nc.scalar.copy(turned_sb[:, lo:hi], turned[:])
            old_bank = psum.tile([P, hi - lo], F32, name="old_bank%d" % n)
            for c in range(0, hi - lo, P):
                nc.tensor.transpose(old_bank[:, c : c + P], turned_sb[:, lo + c : lo + c + P], ident[:])
            old_banks.append(old_bank)

        totals = sb.tile([P, T], F32, name="totals", tag="totals")
        for n, (lo, hi) in enumerate(VECTOR_ADDS):
            nc.vector.tensor_tensor(totals[:, lo:hi], old_banks[n][:], relayed[:, lo:hi], ALU.add)
        nc.gpsimd.tensor_tensor(totals[:, split:], old_gpsimd[:], relayed[:, split:], ALU.add)

        shares = VECTOR_ADDS + [GPSIMD_ADD]
        share_max = sb.tile([P, len(shares)], F32, name="share_max")
        for n, (lo, hi) in enumerate(shares):
            nc.vector.tensor_reduce(share_max[:, n : n + 1], totals[:, lo:hi], FREE_AXIS, ALU.max)
        neg_max = sb.tile([P, 1], F32, name="neg_max")
        nc.vector.tensor_reduce(neg_max[:], share_max[:], FREE_AXIS, ALU.max, negate=True)

        for h in range(2):
            result = sb.tile([P, HALF], F32, name="result%d" % h)
            nc.scalar.activation(
                result[:], totals[:].indirect(fetch_list[:, HALF_LIST[h]]), ACT.Exp, bias=neg_max[:]
            )
            nc.sync.dma_start(out=out[:, h * HALF : (h + 1) * HALF], in_=result[:])
